import numpy as np
import ml_dtypes


def mxq(x, axis, fmt="e4m3"):
    dtype, down = {"e4m3": (ml_dtypes.float8_e4m3fn, 7), "e5m2": (ml_dtypes.float8_e5m2, 14)}[fmt]
    v = np.moveaxis(np.asarray(x, np.float32).astype(ml_dtypes.bfloat16).astype(np.float64), axis, -1)
    blocks = v.reshape(v.shape[:-1] + (-1, 32))
    amax = np.abs(blocks).max(-1, keepdims=True)
    byte = np.maximum(np.where(amax > 0, np.frexp(amax)[1] - 1 + 127, 0) - down, 1)
    scale = np.exp2(byte - 127.0)
    codes = (blocks / scale).astype(np.float32).astype(dtype).astype(np.float64)
    return np.moveaxis((codes * scale).reshape(v.shape), -1, axis)


WIDE = False


def mx_kscale(k):
    if not WIDE:
        return np.ones(k)
    levels = np.array([10, -10, 5, -5, 0])
    if k % 512:
        return np.exp2(np.random.permutation(np.resize(levels, k // 32))).repeat(32)
    a = np.empty((k // 512, 16))
    for p in range(k // 512):
        a[p, :8] = np.random.permutation(np.resize(levels, 8))
        for g in range(8):
            far = levels[np.abs(levels - a[p, g]) >= 10]
            a[p, g + 8] = far[np.random.randint(len(far))]
    return np.exp2(a.ravel()).repeat(32)


def f64(x):
    return np.asarray(x).astype(np.float64)


def striped(idx):
    return np.tile(np.asarray(idx).reshape(-1, 16).T, (8, 1)).astype(np.uint16)


def unstriped(offs):
    return offs[:16].T.reshape(-1).astype(np.int64)


E2M1 = np.array([0.0, 0.5, 1.0, 1.5, 2.0, 3.0, 4.0, 6.0, -0.0, -0.5, -1.0, -1.5, -2.0, -3.0, -4.0, -6.0])


def pack_weight(w, fmt):
    k, n = w.shape
    w = f64(np.asarray(w, np.float32).astype(ml_dtypes.bfloat16)).reshape(k // 32, 32, n)
    amax = np.abs(w).max(1)
    if fmt == "e4m3":
        byte = np.frexp(amax)[1] - 1 + 127 - 7
    else:
        mant, ex = np.frexp(amax / 6.0)
        byte = np.where(mant > 0.5, ex, ex - 1) + 127
    byte = np.clip(np.where(amax > 0, byte, 1), 1, 254)
    scaled = (w * np.exp2(127.0 - byte)[:, None, :]).reshape(k, n).astype(np.float32)
    by_word = np.ascontiguousarray(scaled.reshape(k // 512, 128, 4, n).transpose(0, 1, 3, 2))
    if fmt == "e4m3":
        words = by_word.astype(ml_dtypes.float8_e4m3fn).view(np.uint8)
    else:
        c = by_word.astype(ml_dtypes.float4_e2m1fn).view(np.uint8) & 0xF
        words = (c[..., 0::2] | (c[..., 1::2] << 4)).reshape(k // 512, 128, 2 * n)
    return np.ascontiguousarray(words), np.ascontiguousarray(byte.astype(np.uint8).reshape(k // 512, 16, n))


def unpack_weight(words, scales, fmt):
    g, _, n = scales.shape
    words = np.ascontiguousarray(words).reshape(g, 128, n, -1)
    if fmt == "e4m3":
        vals = words.view(ml_dtypes.float8_e4m3fn).astype(np.float64)
    else:
        nib = np.empty((g, 128, n, 4), np.uint8)
        nib[..., 0::2] = words & 0xF
        nib[..., 1::2] = words >> 4
        vals = E2M1[nib]
    vals = vals * np.repeat(np.exp2(scales.astype(np.float64) - 127.0), 8, axis=1)[..., None]
    return vals.transpose(0, 1, 3, 2).reshape(g * 512, n)


def softplus(v):
    return np.log(1.0 + np.exp(v))


D, K, R, T, I, Q = 512, 512, 512, 1024, 256, 512


def setup_inputs():
    n = np.random.standard_normal
    idx = np.random.permutation(T)[:I]
    fd = mx_kscale(D)
    fk = mx_kscale(K)
    fq = mx_kscale(Q)
    keysp = pack_weight(n((D, T)) / fd[:, None], "e2m1")
    tabp = pack_weight(n((K, T)) / fk[:, None], "e2m1")
    return {
        "query": (n((D, Q)) * 0.9 / np.sqrt(D) * fd[:, None]).astype(np.float32),
        "keys_words": keysp[0],
        "keys_scales": keysp[1],
        "th": (np.random.uniform(-0.3, 0.6, (Q, 1))).astype(np.float32),
        "reserve": (np.random.uniform(50.0, 200.0, (Q, 1))).astype(np.float32),
        "tab_words": tabp[0],
        "tab_scales": tabp[1],
        "w1": (n((K, R)) * 1 / np.sqrt(K) * fk[:, None]).astype(np.float32),
        "gain": (np.random.uniform(0.5, 2.0, (R, 1))).astype(np.float32),
        "qs": (np.random.uniform(4.0, 16.0, (Q, 1)) * fq[:, None]).astype(np.float32),
        "grows": (n((Q, R)) / fq[:, None]).astype(np.float32),
        "sg": (np.random.uniform(0.5, 2.0, (1, I))).astype(np.float32),
        "old": (0.4 * n((R, I))).astype(np.float32),
        "offs": striped(idx),
    }


def reference(query, keys_words, keys_scales, th, reserve, tab_words, tab_scales, w1, gain, qs, grows, sg, old, offs):
    idx = unstriped(offs)
    keysu = unpack_weight(keys_words, keys_scales, "e2m1")
    tabu = unpack_weight(tab_words, tab_scales, "e2m1")
    queryq = mxq(f64(query), 0, "e4m3")
    keysidxg = keysu[:, idx]
    a = queryq.T @ keysidxg
    p = softplus(a - f64(th))
    z = np.sum(p, axis=1, keepdims=True) + f64(reserve)
    w = p / z
    wq = w * f64(qs)
    w1q = mxq(f64(w1), 0, "e4m3")
    tabidxg = tabu[:, idx]
    zh = w1q.T @ tabidxg
    ht = np.tanh(zh)
    growsq = mxq(f64(grows), 0, "e4m3")
    wqq = mxq(wq, 0, "e4m3")
    c0 = growsq.T @ wqq
    dht = c0 * f64(gain)
    dzh = dht * (1.0 - np.square(ht))
    y = dzh * f64(sg) + f64(old)
    return y

@@ -1,0 +1,208 @@
+from contextlib import ExitStack
+
+import concourse.mybir as mybir
+from concourse.masks import make_identity
+
+D, K, R, T, I, Q = 512, 512, 512, 1024, 256, 512
+FLOPS = 2 * I * (D * Q + K * R + Q * R)
+
+F32 = mybir.dt.float32
+BF16 = mybir.dt.bfloat16
+I32 = mybir.dt.int32
+U32 = mybir.dt.uint32
+U16 = mybir.dt.uint16
+U8 = mybir.dt.uint8
+FP8X4 = mybir.dt.float8_e4m3fn_x4
+FP4X4 = mybir.dt.float4_e2m1fn_x4
+ACT = mybir.ActivationFunctionType
+ALU = mybir.AluOpType
+
+P = 128
+PACK = 4
+VECTOR_COLUMNS = 84
+FLOOR_ARG = -30.0
+
+
+def tile_attend_bzgained_capped_kernel(tc, query, keys_words, keys_scales, th, reserve, tab_words, tab_scales, w1, gain, qs, grows, sg, old, offs, out):
+    nc = tc.nc
+    with ExitStack() as ctx:
+        sb = ctx.enter_context(tc.tile_pool(name="sb", bufs=1))
+        ps = ctx.enter_context(tc.psum_pool(name="ps", bufs=1))
+
+        def tile(name, shape, dtype, after=None):
+            return sb.tile(shape, dtype, name=name, tag=after or name, align_bytes=64)
+
+        offsets = sb.tile([P, I // 16], U16, name="offsets")
+        nc.sync.dma_start(offsets[:], offs)
+
+        def load_words(name, words):
+            pool_words = tile(name, [P, T], U16)
+            nc.sync.dma_start(pool_words[:].bitcast(I32), words[0].bitcast(I32))
+            return pool_words
+
+        def zeroed_scales(name):
+            pool_scales = tile(name, [P, T], U8)
+            nc.gpsimd.memset(pool_scales[:].bitcast(I32), 0)
+            return pool_scales
+
+        def load_scale_rows(pool_scales, scales, quad, queue):
+            queue.dma_start(pool_scales[32 * quad : 32 * quad + 4, :].bitcast(I32), scales[0][4 * quad : 4 * quad + 4, :].bitcast(I32))
+
+        def load_rows(name, matrix, queue, after=None):
+            raw = tile(name, [P, PACK, matrix.shape[1]], F32, after)
+            queue.dma_start(raw[:], matrix.rearrange("(p j) c -> p j c", j=PACK))
+            return raw
+
+        def load_by_row(name, column):
+            vec = tile(name, [P, PACK], F32)
+            nc.gpsimd.dma_start(vec[:], column.rearrange("(p t) o -> p (t o)", t=PACK))
+            return vec
+
+        keys_pool_scales = zeroed_scales("keys_scales")
+        tab_pool_scales = zeroed_scales("tab_scales")
+        for quad in range(4):
+            load_scale_rows(keys_pool_scales, keys_scales, quad, nc.scalar)
+        keys_pool = (load_words("keys_words", keys_words), keys_pool_scales)
+        load_scale_rows(tab_pool_scales, tab_scales, 0, nc.sync)
+        query_raw = load_rows("query_raw", query, nc.sync, "query_raw")
+        tab_pool = (load_words("tab_words", tab_words), tab_pool_scales)
+        for quad in range(1, 4):
+            load_scale_rows(tab_pool_scales, tab_scales, quad, nc.sync)
+        w1_raw = load_rows("w1_raw", w1, nc.sync)
+        grows_raw = load_rows("grows_raw", grows, nc.sync)
+        old_sb = tile("old_sb", [P, 2, 2 * I], F32)
+        nc.sync.dma_start(old_sb[:], old.rearrange("(h p e) i -> p h (e i)", h=2, e=2))
+        th_sb = load_by_row("th_sb", th)
+        reserve_sb = load_by_row("reserve_sb", reserve)
+        qs_sb = load_by_row("qs_sb", qs)
+        ident = tile("ident", [P, P], F32)
+        make_identity(nc, ident[:])
+        sg_col = tile("sg_col", [P, 2], F32)
+        nc.gpsimd.dma_start(sg_col[:], sg.rearrange("o (p u) -> p (o u)", u=2))
+        gain_sb = tile("gain_sb", [P, 2, 2], F32)
+        nc.gpsimd.dma_start(gain_sb[:], gain.rearrange("(h p e) o -> p h (e o)", h=2, e=2))
+
+        floor_arg = tile("floor_arg", [P, 1], F32)
+        nc.vector.memset(floor_arg[:], FLOOR_ARG)
+        floor = tile("floor", [P, 1], F32)
+        nc.scalar.activation(floor[:], floor_arg[:], ACT.Sigmoid)
+
+        def gather(name, pool):
+            words = tile(name + "_listed_words", [P, I], U16)
+            scales = tile(name + "_listed_scales", [P, I], U8)
+            nc.vector.tensor_copy(words[:], pool[0][:].indirect(offsets[:]))
+            nc.vector.tensor_copy(scales[:], pool[1][:].indirect(offsets[:]))
+            return words, scales
+
+        keys_listed = gather("keys", keys_pool)
+
+        query_bf = tile("query_bf", [P, PACK, P, PACK], BF16)
+        dst = query_bf[:].rearrange("p t m j -> p m t j")
+        src = query_raw[:].rearrange("p j (m t) -> p m t j", t=PACK)
+        nc.vector.tensor_scalar(dst[:, :VECTOR_COLUMNS], src[:, :VECTOR_COLUMNS], -1.0, None, ALU.mult)
+        nc.scalar.activation(dst[:, VECTOR_COLUMNS:], src[:, VECTOR_COLUMNS:], ACT.Copy, scale=-1.0)
+        query_words = tile("query_words", [P, Q], U32)
+        query_scales = tile("query_scales", [P, Q], U8)
+        work = tile("work", [P, PACK, I], F32)
+        scores = []
+        for t in range(PACK):
+            cols = slice(t * P, (t + 1) * P)
+            nc.vector.quantize_mx(query_words[:, cols].bitcast(FP8X4), query_scales[:, cols], query_bf[:, t].rearrange("p m j -> p (m j)"))
+            score = ps.tile([P, I], F32, name="score%d" % t)
+            nc.tensor.matmul_mx(score[:], lhsT=query_words[:, cols].bitcast(FP8X4), lhsT_scale=query_scales[:, cols], rhs=keys_listed[0][:].bitcast(FP4X4), rhs_scale=keys_listed[1][:], start=True, stop=True)
+            nc.scalar.activation(work[:, t, :], score[:], ACT.Sigmoid, bias=th_sb[:, t : t + 1])
+            scores.append(score)
+
+        tab_listed = gather("tab", tab_pool)
+
+        def operand_tiles(name):
+            return tile(name + "_bf", [P, 2, 2, P, PACK], BF16), tile(name + "_words", [P, R], U32), tile(name + "_scales", [P, R], U8)
+
+        def cast_half(tiles, raw, h, copy):
+            copy(
+                tiles[0][:, h].rearrange("p e (c n) j -> p c j n e", n=2),
+                raw[:, :, 256 * h : 256 * (h + 1)].rearrange("p j (c n e) -> p c j n e", n=2, e=2),
+            )
+
+        def quantize_half(tiles, h):
+            cols = slice(256 * h, 256 * (h + 1))
+            nc.vector.quantize_mx(tiles[1][:, cols].bitcast(FP8X4), tiles[2][:, cols], tiles[0][:, h].rearrange("p e m j -> p (e m j)"))
+
+        def product_half(bank, tiles, h, moving_words, moving_scales):
+            for e in range(2):
+                cols = slice(256 * h + P * e, 256 * h + P * (e + 1))
+                nc.tensor.matmul_mx(bank[:, e, :], lhsT=tiles[1][:, cols].bitcast(FP8X4), lhsT_scale=tiles[2][:, cols], rhs=moving_words, rhs_scale=moving_scales, start=True, stop=True)
+
+        w1_tiles = operand_tiles("w1")
+        grows_tiles = operand_tiles("grows")
+        for h in range(2):
+            cast_half(w1_tiles, w1_raw, h, nc.vector.tensor_copy)
+        zh = []
+        for h in range(2):
+            quantize_half(w1_tiles, h)
+            bank = ps.tile([P, 2, I], F32, name="zh%d" % h)
+            product_half(bank, w1_tiles, h, tab_listed[0][:].bitcast(FP4X4), tab_listed[1][:])
+            zh.append(bank)
+
+        log_outer = tile("log_outer", [P, 2, I], F32)
+        nc.scalar.activation(log_outer[:], work[:, 0:4:3, :], ACT.Ln, bias=floor[:])
+        nc.scalar.activation(work[:, 0:4:3, :], work[:, 1:3, :], ACT.Ln, bias=floor[:])
+        logs = (log_outer[:, 0, :], work[:, 0, :], work[:, 3, :], log_outer[:, 1, :])
+
+        cast_half(grows_tiles, grows_raw, 1, nc.scalar.copy)
+
+        neg_p = tile("neg_p", [P, PACK, I], F32, "w1_raw")
+        neg_sum = tile("neg_sum", [P, PACK], F32)
+        for t in (0, 3, 1, 2):
+            nc.vector.scalar_tensor_tensor(neg_p[:, t, :], scores[t][:], th_sb[:, t : t + 1], logs[t], ALU.add, ALU.min, accum_out=neg_sum[:, t : t + 1])
+        neg_z = tile("neg_z", [P, PACK], F32)
+        nc.vector.tensor_tensor(neg_z[:], neg_sum[:], reserve_sb[:], ALU.subtract)
+        neg_inv = tile("neg_inv", [P, PACK], F32)
+        nc.vector.reciprocal(neg_inv[:], neg_z[:])
+        neg_factor = tile("neg_factor", [P, PACK], F32)
+        nc.vector.tensor_tensor(neg_factor[:], neg_inv[:], qs_sb[:], ALU.mult)
+
+        cast_half(grows_tiles, grows_raw, 0, nc.vector.tensor_copy)
+
+        wq_bf = tile("wq_bf", [P, I, PACK], BF16)
+        wq_words = tile("wq_words", [P, I], U32)
+        wq_scales = tile("wq_scales", [P, I], U8)
+        for u in range(2):
+            slots = slice(P * u, P * (u + 1))
+            nc.vector.tensor_tensor(
+                wq_bf[:, slots, :].rearrange("p (c n) t -> p c t n", n=4),
+                neg_p[:, :, slots].rearrange("p t (c n) -> p c t n", n=4),
+                neg_factor[:].unsqueeze(1).unsqueeze(3).to_broadcast([P, P // 4, PACK, 4]),
+                ALU.mult,
+            )
+        for u in range(2):
+            slots = slice(P * u, P * (u + 1))
+            nc.vector.quantize_mx(wq_words[:, slots].bitcast(FP8X4), wq_scales[:, slots], wq_bf[:, slots, :].rearrange("p i t -> p (i t)"))
+        for h in range(2):
+            quantize_half(grows_tiles, h)
+
+        sg_ps = ps.tile([P, 2, P], F32, name="sg_ps", tag="c0_0")
+        for u in range(2):
+            nc.tensor.transpose(sg_ps[:, u, :], sg_col[:, u : u + 1].to_broadcast([P, P]), ident[:])
+        sg_rows = tile("sg_rows", [P, I], F32)
+        nc.scalar.copy(sg_rows[:].rearrange("p (m u) -> p m u", u=2), sg_ps[:].rearrange("p u m -> p m u"))
+
+        slope = tile("slope", [P, 2, 2 * I], F32)
+        squares = tile("squares", [P, 2, 2 * I], F32)
+        for h in range(2):
+            ht = grows_raw[:, 2 * h : 2 * h + 2, 256:]
+            nc.scalar.activation(ht, zh[h][:], ACT.Tanh)
+            nc.scalar.activation(squares[:, h, :].rearrange("p (e i) -> p e i", e=2), ht, ACT.Square)
+            nc.vector.scalar_tensor_tensor(slope[:, h, :].rearrange("p (e i) -> p e i", e=2), squares[:, h, :].rearrange("p (e i) -> p e i", e=2), 1.0, sg_rows[:].unsqueeze(1).to_broadcast([P, 2, I]), ALU.subtract, ALU.mult)
+
+        out_rows = out.rearrange("(h p e) i -> p h (e i)", h=2, e=2)
+        term = tile("term", [P, 2, 2 * I], F32)
+        result = tile("result", [P, 2, 2 * I], F32)
+        for h in range(2):
+            c0 = ps.tile([P, 2, I], F32, name="c0_%d" % h, tag="c0_%d" % h)
+            product_half(c0, grows_tiles, h, wq_words[:].bitcast(FP8X4), wq_scales[:])
+            for e in range(2):
+                cols = slice(I * e, I * (e + 1))
+                nc.vector.scalar_tensor_tensor(term[:, h, cols], c0[:, e, :], gain_sb[:, h, e : e + 1], slope[:, h, cols], ALU.mult, ALU.mult)
+            nc.vector.tensor_tensor(result[:, h, :], old_sb[:, h, :], term[:, h, :], ALU.subtract)
+            nc.sync.dma_start(out_rows[:, h, :], result[:, h, :])

@@ -19,7 +19,7 @@ ALU = mybir.AluOpType
 
 P = 128
 PACK = 4
-VECTOR_COLUMNS = 84
+VECTOR_COLUMNS = 88
 FLOOR_ARG = -30.0
 
 
@@ -53,52 +53,53 @@ def tile_attend_bzgained_capped_kernel(tc, query, keys_words, keys_scales, th, r
             queue.dma_start(raw[:], matrix.rearrange("(p j) c -> p j c", j=PACK))
             return raw
 
-        def load_by_row(name, column):
+        def load_halves(name, matrix):
+            return [load_rows("%s%d" % (name, h), matrix[:, 256 * h : 256 * (h + 1)], nc.sync) for h in range(2)]
+
+        def load_by_row(name, column, queue):
             vec = tile(name, [P, PACK], F32)
-            nc.gpsimd.dma_start(vec[:], column.rearrange("(p t) o -> p (t o)", t=PACK))
+            queue.dma_start(vec[:], column.rearrange("(p t) o -> p (t o)", t=PACK))
             return vec
 
         keys_pool_scales = zeroed_scales("keys_scales")
         tab_pool_scales = zeroed_scales("tab_scales")
+        floor_arg = tile("floor_arg", [P, 1], F32)
+        nc.gpsimd.memset(floor_arg[:], FLOOR_ARG)
+        th_sb = load_by_row("th_sb", th, nc.gpsimd)
+        ident = tile("ident", [P, P], F32)
+        make_identity(nc, ident[:])
         for quad in range(4):
             load_scale_rows(keys_pool_scales, keys_scales, quad, nc.scalar)
         keys_pool = (load_words("keys_words", keys_words), keys_pool_scales)
-        load_scale_rows(tab_pool_scales, tab_scales, 0, nc.sync)
-        query_raw = load_rows("query_raw", query, nc.sync, "query_raw")
         tab_pool = (load_words("tab_words", tab_words), tab_pool_scales)
-        for quad in range(1, 4):
+        query_raw = load_rows("query_raw", query, nc.sync)
+        w1_raw = load_halves("w1_raw", w1)
+        for quad in range(4):
             load_scale_rows(tab_pool_scales, tab_scales, quad, nc.sync)
-        w1_raw = load_rows("w1_raw", w1, nc.sync)
-        grows_raw = load_rows("grows_raw", grows, nc.sync)
+        grows_raw = load_halves("grows_raw", grows)
+        reserve_sb = load_by_row("reserve_sb", reserve, nc.sync)
+        qs_sb = load_by_row("qs_sb", qs, nc.sync)
+        sg_col = tile("sg_col", [P, 2], F32)
+        nc.sync.dma_start(sg_col[:], sg.rearrange("o (p u) -> p (o u)", u=2))
+        gain_sb = tile("gain_sb", [P, 2, 2], F32)
+        nc.sync.dma_start(gain_sb[:], gain.rearrange("(h p e) o -> p h (e o)", h=2, e=2))
         old_sb = tile("old_sb", [P, 2, 2 * I], F32)
         nc.sync.dma_start(old_sb[:], old.rearrange("(h p e) i -> p h (e i)", h=2, e=2))
-        th_sb = load_by_row("th_sb", th)
-        reserve_sb = load_by_row("reserve_sb", reserve)
-        qs_sb = load_by_row("qs_sb", qs)
-        ident = tile("ident", [P, P], F32)
-        make_identity(nc, ident[:])
-        sg_col = tile("sg_col", [P, 2], F32)
-        nc.gpsimd.dma_start(sg_col[:], sg.rearrange("o (p u) -> p (o u)", u=2))
-        gain_sb = tile("gain_sb", [P, 2, 2], F32)
-        nc.gpsimd.dma_start(gain_sb[:], gain.rearrange("(h p e) o -> p h (e o)", h=2, e=2))
 
-        floor_arg = tile("floor_arg", [P, 1], F32)
-        nc.vector.memset(floor_arg[:], FLOOR_ARG)
         floor = tile("floor", [P, 1], F32)
         nc.scalar.activation(floor[:], floor_arg[:], ACT.Sigmoid)
 
-        def gather(name, pool):
-            words = tile(name + "_listed_words", [P, I], U16)
-            scales = tile(name + "_listed_scales", [P, I], U8)
-            nc.vector.tensor_copy(words[:], pool[0][:].indirect(offsets[:]))
-            nc.vector.tensor_copy(scales[:], pool[1][:].indirect(offsets[:]))
-            return words, scales
+        def gather(name, pool, dtype):
+            listed = tile(name, [P, I], dtype)
+            nc.vector.tensor_copy(listed[:], pool[:].indirect(offsets[:]))
+            return listed
 
-        keys_listed = gather("keys", keys_pool)
+        keys_listed = (gather("keys_listed_words", keys_pool[0], U16), gather("keys_listed_scales", keys_pool[1], U8))
+        tab_listed_words = gather("tab_listed_words", tab_pool[0], U16)
 
-        query_bf = tile("query_bf", [P, PACK, P, PACK], BF16)
-        dst = query_bf[:].rearrange("p t m j -> p m t j")
-        src = query_raw[:].rearrange("p j (m t) -> p m t j", t=PACK)
+        query_bf = tile("query_bf", [P, PACK, P, PACK], BF16, "keys_scales")
+        dst = query_bf[:].rearrange("p t m j -> p m j t")
+        src = query_raw[:].rearrange("p j (m t) -> p m j t", t=PACK)
         nc.vector.tensor_scalar(dst[:, :VECTOR_COLUMNS], src[:, :VECTOR_COLUMNS], -1.0, None, ALU.mult)
         nc.scalar.activation(dst[:, VECTOR_COLUMNS:], src[:, VECTOR_COLUMNS:], ACT.Copy, scale=-1.0)
         query_words = tile("query_words", [P, Q], U32)
@@ -113,15 +114,13 @@ def tile_attend_bzgained_capped_kernel(tc, query, keys_words, keys_scales, th, r
             nc.scalar.activation(work[:, t, :], score[:], ACT.Sigmoid, bias=th_sb[:, t : t + 1])
             scores.append(score)
 
-        tab_listed = gather("tab", tab_pool)
-
         def operand_tiles(name):
             return tile(name + "_bf", [P, 2, 2, P, PACK], BF16), tile(name + "_words", [P, R], U32), tile(name + "_scales", [P, R], U8)
 
-        def cast_half(tiles, raw, h, copy):
-            copy(
+        def cast_half(tiles, raw_half, h):
+            nc.vector.tensor_copy(
                 tiles[0][:, h].rearrange("p e (c n) j -> p c j n e", n=2),
-                raw[:, :, 256 * h : 256 * (h + 1)].rearrange("p j (c n e) -> p c j n e", n=2, e=2),
+                raw_half.rearrange("p j (c n e) -> p c j n e", n=2, e=2),
             )
 
         def quantize_half(tiles, h):
@@ -136,10 +135,12 @@ def tile_attend_bzgained_capped_kernel(tc, query, keys_words, keys_scales, th, r
         w1_tiles = operand_tiles("w1")
         grows_tiles = operand_tiles("grows")
         for h in range(2):
-            cast_half(w1_tiles, w1_raw, h, nc.vector.tensor_copy)
-        zh = []
+            cast_half(w1_tiles, w1_raw[h][:], h)
         for h in range(2):
             quantize_half(w1_tiles, h)
+        tab_listed = (tab_listed_words, gather("tab_listed_scales", tab_pool[1], U8))
+        zh = []
+        for h in range(2):
             bank = ps.tile([P, 2, I], F32, name="zh%d" % h)
             product_half(bank, w1_tiles, h, tab_listed[0][:].bitcast(FP4X4), tab_listed[1][:])
             zh.append(bank)
@@ -149,9 +150,11 @@ def tile_attend_bzgained_capped_kernel(tc, query, keys_words, keys_scales, th, r
         nc.scalar.activation(work[:, 0:4:3, :], work[:, 1:3, :], ACT.Ln, bias=floor[:])
         logs = (log_outer[:, 0, :], work[:, 0, :], work[:, 3, :], log_outer[:, 1, :])
 
-        cast_half(grows_tiles, grows_raw, 1, nc.scalar.copy)
+        for h in range(2):
+            cast_half(grows_tiles, grows_raw[h][:], h)
+        quantize_half(grows_tiles, 0)
 
-        neg_p = tile("neg_p", [P, PACK, I], F32, "w1_raw")
+        neg_p = tile("neg_p", [P, PACK, I], F32, "grows_raw1")
         neg_sum = tile("neg_sum", [P, PACK], F32)
         for t in (0, 3, 1, 2):
             nc.vector.scalar_tensor_tensor(neg_p[:, t, :], scores[t][:], th_sb[:, t : t + 1], logs[t], ALU.add, ALU.min, accum_out=neg_sum[:, t : t + 1])
@@ -162,7 +165,7 @@ def tile_attend_bzgained_capped_kernel(tc, query, keys_words, keys_scales, th, r
         neg_factor = tile("neg_factor", [P, PACK], F32)
         nc.vector.tensor_tensor(neg_factor[:], neg_inv[:], qs_sb[:], ALU.mult)
 
-        cast_half(grows_tiles, grows_raw, 0, nc.vector.tensor_copy)
+        quantize_half(grows_tiles, 1)
 
         wq_bf = tile("wq_bf", [P, I, PACK], BF16)
         wq_words = tile("wq_words", [P, I], U32)
@@ -178,8 +181,6 @@ def tile_attend_bzgained_capped_kernel(tc, query, keys_words, keys_scales, th, r
         for u in range(2):
             slots = slice(P * u, P * (u + 1))
             nc.vector.quantize_mx(wq_words[:, slots].bitcast(FP8X4), wq_scales[:, slots], wq_bf[:, slots, :].rearrange("p i t -> p (i t)"))
-        for h in range(2):
-            quantize_half(grows_tiles, h)
 
         sg_ps = ps.tile([P, 2, P], F32, name="sg_ps", tag="c0_0")
         for u in range(2):
@@ -187,10 +188,11 @@ def tile_attend_bzgained_capped_kernel(tc, query, keys_words, keys_scales, th, r
         sg_rows = tile("sg_rows", [P, I], F32)
         nc.scalar.copy(sg_rows[:].rearrange("p (m u) -> p m u", u=2), sg_ps[:].rearrange("p u m -> p m u"))
 
-        slope = tile("slope", [P, 2, 2 * I], F32)
+        slope = tile("slope", [P, 2, 2 * I], F32, "grows_raw1")
+        hts = tile("hts", [P, 2, 2, I], F32)
         squares = tile("squares", [P, 2, 2 * I], F32)
         for h in range(2):
-            ht = grows_raw[:, 2 * h : 2 * h + 2, 256:]
+            ht = hts[:, h]
             nc.scalar.activation(ht, zh[h][:], ACT.Tanh)
             nc.scalar.activation(squares[:, h, :].rearrange("p (e i) -> p e i", e=2), ht, ACT.Square)
             nc.vector.scalar_tensor_tensor(slope[:, h, :].rearrange("p (e i) -> p e i", e=2), squares[:, h, :].rearrange("p (e i) -> p e i", e=2), 1.0, sg_rows[:].unsqueeze(1).to_broadcast([P, 2, I]), ALU.subtract, ALU.mult)
@@ -204,5 +206,6 @@ def tile_attend_bzgained_capped_kernel(tc, query, keys_words, keys_scales, th, r
             for e in range(2):
                 cols = slice(I * e, I * (e + 1))
                 nc.vector.scalar_tensor_tensor(term[:, h, cols], c0[:, e, :], gain_sb[:, h, e : e + 1], slope[:, h, cols], ALU.mult, ALU.mult)
-            nc.vector.tensor_tensor(result[:, h, :], old_sb[:, h, :], term[:, h, :], ALU.subtract)
-            nc.sync.dma_start(out_rows[:, h, :], result[:, h, :])
+            for cols in ([slice(0, 2 * I)] if h == 0 else [slice(0, I), slice(I, 2 * I)]):
+                nc.vector.tensor_tensor(result[:, h, cols], old_sb[:, h, cols], term[:, h, cols], ALU.subtract)
+                nc.sync.dma_start(out_rows[:, h, cols], result[:, h, cols])

@@ -19,7 +19,7 @@ ALU = mybir.AluOpType
 
 P = 128
 PACK = 4
-VECTOR_COLUMNS = 88
+VECTOR_COLUMNS = 44
 FLOOR_ARG = -30.0
 
 
@@ -40,13 +40,12 @@ def tile_attend_bzgained_capped_kernel(tc, query, keys_words, keys_scales, th, r
             nc.sync.dma_start(pool_words[:].bitcast(I32), words[0].bitcast(I32))
             return pool_words
 
-        def zeroed_scales(name):
+        def load_scales(name, scales):
             pool_scales = tile(name, [P, T], U8)
-            nc.gpsimd.memset(pool_scales[:].bitcast(I32), 0)
+            for quad in range(4):
+                rows = scales[0][4 * quad : 4 * quad + 4, :].bitcast(I32)
+                nc.sync.dma_start(pool_scales[32 * quad : 32 * (quad + 1), :].bitcast(I32), rows.unsqueeze(0).to_broadcast([8, 4, T // 4]))
             return pool_scales
-
-        def load_scale_rows(pool_scales, scales, quad, queue):
-            queue.dma_start(pool_scales[32 * quad : 32 * quad + 4, :].bitcast(I32), scales[0][4 * quad : 4 * quad + 4, :].bitcast(I32))
 
         def load_rows(name, matrix, queue, after=None):
             raw = tile(name, [P, PACK, matrix.shape[1]], F32, after)
@@ -61,26 +60,21 @@ def tile_attend_bzgained_capped_kernel(tc, query, keys_words, keys_scales, th, r
             queue.dma_start(vec[:], column.rearrange("(p t) o -> p (t o)", t=PACK))
             return vec
 
-        keys_pool_scales = zeroed_scales("keys_scales")
-        tab_pool_scales = zeroed_scales("tab_scales")
         floor_arg = tile("floor_arg", [P, 1], F32)
         nc.gpsimd.memset(floor_arg[:], FLOOR_ARG)
-        th_sb = load_by_row("th_sb", th, nc.gpsimd)
         ident = tile("ident", [P, P], F32)
         make_identity(nc, ident[:])
-        for quad in range(4):
-            load_scale_rows(keys_pool_scales, keys_scales, quad, nc.scalar)
+        keys_pool_scales = load_scales("keys_scales", keys_scales)
         keys_pool = (load_words("keys_words", keys_words), keys_pool_scales)
-        tab_pool = (load_words("tab_words", tab_words), tab_pool_scales)
-        query_raw = load_rows("query_raw", query, nc.sync)
+        query_raw = load_halves("query_raw", query)
+        th_sb = load_by_row("th_sb", th, nc.sync)
+        tab_pool = (load_words("tab_words", tab_words), load_scales("tab_scales", tab_scales))
         w1_raw = load_halves("w1_raw", w1)
-        for quad in range(4):
-            load_scale_rows(tab_pool_scales, tab_scales, quad, nc.sync)
+        sg_col = tile("sg_col", [P, 2], F32)
+        nc.sync.dma_start(sg_col[:], sg.rearrange("o (p u) -> p (o u)", u=2))
         grows_raw = load_halves("grows_raw", grows)
         reserve_sb = load_by_row("reserve_sb", reserve, nc.sync)
         qs_sb = load_by_row("qs_sb", qs, nc.sync)
-        sg_col = tile("sg_col", [P, 2], F32)
-        nc.sync.dma_start(sg_col[:], sg.rearrange("o (p u) -> p (o u)", u=2))
         gain_sb = tile("gain_sb", [P, 2, 2], F32)
         nc.sync.dma_start(gain_sb[:], gain.rearrange("(h p e) o -> p h (e o)", h=2, e=2))
         old_sb = tile("old_sb", [P, 2, 2 * I], F32)
@@ -95,13 +89,14 @@ def tile_attend_bzgained_capped_kernel(tc, query, keys_words, keys_scales, th, r
             return listed
 
         keys_listed = (gather("keys_listed_words", keys_pool[0], U16), gather("keys_listed_scales", keys_pool[1], U8))
-        tab_listed_words = gather("tab_listed_words", tab_pool[0], U16)
 
-        query_bf = tile("query_bf", [P, PACK, P, PACK], BF16, "keys_scales")
+        query_bf = tile("query_bf", [P, PACK, P, PACK], BF16)
         dst = query_bf[:].rearrange("p t m j -> p m j t")
-        src = query_raw[:].rearrange("p j (m t) -> p m j t", t=PACK)
-        nc.vector.tensor_scalar(dst[:, :VECTOR_COLUMNS], src[:, :VECTOR_COLUMNS], -1.0, None, ALU.mult)
-        nc.scalar.activation(dst[:, VECTOR_COLUMNS:], src[:, VECTOR_COLUMNS:], ACT.Copy, scale=-1.0)
+        for h in range(2):
+            src = query_raw[h][:].rearrange("p j (m t) -> p m j t", t=PACK)
+            split = 64 * h + VECTOR_COLUMNS
+            nc.vector.tensor_scalar(dst[:, 64 * h : split], src[:, :VECTOR_COLUMNS], -1.0, None, ALU.mult)
+            nc.scalar.activation(dst[:, split : 64 * (h + 1)], src[:, VECTOR_COLUMNS:], ACT.Copy, scale=-1.0)
         query_words = tile("query_words", [P, Q], U32)
         query_scales = tile("query_scales", [P, Q], U8)
         work = tile("work", [P, PACK, I], F32)
@@ -114,11 +109,13 @@ def tile_attend_bzgained_capped_kernel(tc, query, keys_words, keys_scales, th, r
             nc.scalar.activation(work[:, t, :], score[:], ACT.Sigmoid, bias=th_sb[:, t : t + 1])
             scores.append(score)
 
+        tab_listed = (gather("tab_listed_words", tab_pool[0], U16), gather("tab_listed_scales", tab_pool[1], U8))
+
         def operand_tiles(name):
             return tile(name + "_bf", [P, 2, 2, P, PACK], BF16), tile(name + "_words", [P, R], U32), tile(name + "_scales", [P, R], U8)
 
-        def cast_half(tiles, raw_half, h):
-            nc.vector.tensor_copy(
+        def cast_half(tiles, raw_half, h, copy):
+            copy(
                 tiles[0][:, h].rearrange("p e (c n) j -> p c j n e", n=2),
                 raw_half.rearrange("p j (c n e) -> p c j n e", n=2, e=2),
             )
@@ -135,10 +132,9 @@ def tile_attend_bzgained_capped_kernel(tc, query, keys_words, keys_scales, th, r
         w1_tiles = operand_tiles("w1")
         grows_tiles = operand_tiles("grows")
         for h in range(2):
-            cast_half(w1_tiles, w1_raw[h][:], h)
+            cast_half(w1_tiles, w1_raw[h][:], h, nc.vector.tensor_copy)
         for h in range(2):
             quantize_half(w1_tiles, h)
-        tab_listed = (tab_listed_words, gather("tab_listed_scales", tab_pool[1], U8))
         zh = []
         for h in range(2):
             bank = ps.tile([P, 2, I], F32, name="zh%d" % h)
@@ -150,11 +146,11 @@ def tile_attend_bzgained_capped_kernel(tc, query, keys_words, keys_scales, th, r
         nc.scalar.activation(work[:, 0:4:3, :], work[:, 1:3, :], ACT.Ln, bias=floor[:])
         logs = (log_outer[:, 0, :], work[:, 0, :], work[:, 3, :], log_outer[:, 1, :])
 
-        for h in range(2):
-            cast_half(grows_tiles, grows_raw[h][:], h)
+        cast_half(grows_tiles, grows_raw[0][:], 0, nc.vector.tensor_copy)
+        cast_half(grows_tiles, grows_raw[1][:], 1, nc.scalar.copy)
         quantize_half(grows_tiles, 0)
 
-        neg_p = tile("neg_p", [P, PACK, I], F32, "grows_raw1")
+        neg_p = tile("neg_p", [P, PACK, I], F32, "grows_raw0")
         neg_sum = tile("neg_sum", [P, PACK], F32)
         for t in (0, 3, 1, 2):
             nc.vector.scalar_tensor_tensor(neg_p[:, t, :], scores[t][:], th_sb[:, t : t + 1], logs[t], ALU.add, ALU.min, accum_out=neg_sum[:, t : t + 1])
@@ -164,8 +160,6 @@ def tile_attend_bzgained_capped_kernel(tc, query, keys_words, keys_scales, th, r
         nc.vector.reciprocal(neg_inv[:], neg_z[:])
         neg_factor = tile("neg_factor", [P, PACK], F32)
         nc.vector.tensor_tensor(neg_factor[:], neg_inv[:], qs_sb[:], ALU.mult)
-
-        quantize_half(grows_tiles, 1)
 
         wq_bf = tile("wq_bf", [P, I, PACK], BF16)
         wq_words = tile("wq_words", [P, I], U32)
@@ -181,6 +175,7 @@ def tile_attend_bzgained_capped_kernel(tc, query, keys_words, keys_scales, th, r
         for u in range(2):
             slots = slice(P * u, P * (u + 1))
             nc.vector.quantize_mx(wq_words[:, slots].bitcast(FP8X4), wq_scales[:, slots], wq_bf[:, slots, :].rearrange("p i t -> p (i t)"))
+        quantize_half(grows_tiles, 1)
 
         sg_ps = ps.tile([P, 2, P], F32, name="sg_ps", tag="c0_0")
         for u in range(2):
@@ -188,8 +183,8 @@ def tile_attend_bzgained_capped_kernel(tc, query, keys_words, keys_scales, th, r
         sg_rows = tile("sg_rows", [P, I], F32)
         nc.scalar.copy(sg_rows[:].rearrange("p (m u) -> p m u", u=2), sg_ps[:].rearrange("p u m -> p m u"))
 
-        slope = tile("slope", [P, 2, 2 * I], F32, "grows_raw1")
-        hts = tile("hts", [P, 2, 2, I], F32)
+        slope = tile("slope", [P, 2, 2 * I], F32, "grows_raw0")
+        hts = tile("hts", [P, 2, 2, I], F32, "grows_raw1")
         squares = tile("squares", [P, 2, 2 * I], F32)
         for h in range(2):
             ht = hts[:, h]

@@ -19,7 +19,7 @@ ALU = mybir.AluOpType
 
 P = 128
 PACK = 4
-VECTOR_COLUMNS = 44
+VECTOR_COLUMNS = 88
 FLOOR_ARG = -30.0
 
 
@@ -66,10 +66,10 @@ def tile_attend_bzgained_capped_kernel(tc, query, keys_words, keys_scales, th, r
         make_identity(nc, ident[:])
         keys_pool_scales = load_scales("keys_scales", keys_scales)
         keys_pool = (load_words("keys_words", keys_words), keys_pool_scales)
-        query_raw = load_halves("query_raw", query)
+        query_raw = load_rows("query_raw", query, nc.sync)
         th_sb = load_by_row("th_sb", th, nc.sync)
         tab_pool = (load_words("tab_words", tab_words), load_scales("tab_scales", tab_scales))
-        w1_raw = load_halves("w1_raw", w1)
+        w1_raw = load_rows("w1_raw", w1, nc.sync)
         sg_col = tile("sg_col", [P, 2], F32)
         nc.sync.dma_start(sg_col[:], sg.rearrange("o (p u) -> p (o u)", u=2))
         grows_raw = load_halves("grows_raw", grows)
@@ -92,11 +92,9 @@ def tile_attend_bzgained_capped_kernel(tc, query, keys_words, keys_scales, th, r
 
         query_bf = tile("query_bf", [P, PACK, P, PACK], BF16)
         dst = query_bf[:].rearrange("p t m j -> p m j t")
-        for h in range(2):
-            src = query_raw[h][:].rearrange("p j (m t) -> p m j t", t=PACK)
-            split = 64 * h + VECTOR_COLUMNS
-            nc.vector.tensor_scalar(dst[:, 64 * h : split], src[:, :VECTOR_COLUMNS], -1.0, None, ALU.mult)
-            nc.scalar.activation(dst[:, split : 64 * (h + 1)], src[:, VECTOR_COLUMNS:], ACT.Copy, scale=-1.0)
+        src = query_raw[:].rearrange("p j (m t) -> p m j t", t=PACK)
+        nc.vector.tensor_scalar(dst[:, :VECTOR_COLUMNS], src[:, :VECTOR_COLUMNS], -1.0, None, ALU.mult)
+        nc.scalar.activation(dst[:, VECTOR_COLUMNS:], src[:, VECTOR_COLUMNS:], ACT.Copy, scale=-1.0)
         query_words = tile("query_words", [P, Q], U32)
         query_scales = tile("query_scales", [P, Q], U8)
         work = tile("work", [P, PACK, I], F32)
@@ -132,7 +130,7 @@ def tile_attend_bzgained_capped_kernel(tc, query, keys_words, keys_scales, th, r
         w1_tiles = operand_tiles("w1")
         grows_tiles = operand_tiles("grows")
         for h in range(2):
-            cast_half(w1_tiles, w1_raw[h][:], h, nc.vector.tensor_copy)
+            cast_half(w1_tiles, w1_raw[:, :, 256 * h : 256 * (h + 1)], h, nc.vector.tensor_copy)
         for h in range(2):
             quantize_half(w1_tiles, h)
         zh = []

from contextlib import ExitStack

import concourse.mybir as mybir
from concourse.masks import make_identity

D, K, R, T, I, Q = 512, 512, 512, 1024, 256, 512
FLOPS = 2 * I * (D * Q + K * R + Q * R)

F32 = mybir.dt.float32
BF16 = mybir.dt.bfloat16
I32 = mybir.dt.int32
U32 = mybir.dt.uint32
U16 = mybir.dt.uint16
U8 = mybir.dt.uint8
FP8X4 = mybir.dt.float8_e4m3fn_x4
FP4X4 = mybir.dt.float4_e2m1fn_x4
ACT = mybir.ActivationFunctionType
ALU = mybir.AluOpType

P = 128
PACK = 4
VECTOR_COLUMNS = 88
FLOOR_ARG = -30.0


def tile_attend_bzgained_capped_kernel(tc, query, keys_words, keys_scales, th, reserve, tab_words, tab_scales, w1, gain, qs, grows, sg, old, offs, out):
    nc = tc.nc
    with ExitStack() as ctx:
        sb = ctx.enter_context(tc.tile_pool(name="sb", bufs=1))
        ps = ctx.enter_context(tc.psum_pool(name="ps", bufs=1))

        def tile(name, shape, dtype, after=None):
            return sb.tile(shape, dtype, name=name, tag=after or name, align_bytes=64)

        offsets = sb.tile([P, I // 16], U16, name="offsets")
        nc.sync.dma_start(offsets[:], offs)

        def load_words(name, words):
            pool_words = tile(name, [P, T], U16)
            nc.sync.dma_start(pool_words[:].bitcast(I32), words[0].bitcast(I32))
            return pool_words

        def load_scales(name, scales):
            pool_scales = tile(name, [P, T], U8)
            for quad in range(4):
                rows = scales[0][4 * quad : 4 * quad + 4, :].bitcast(I32)
                nc.sync.dma_start(pool_scales[32 * quad : 32 * (quad + 1), :].bitcast(I32), rows.unsqueeze(0).to_broadcast([8, 4, T // 4]))
            return pool_scales

        def load_rows(name, matrix, queue, after=None):
            raw = tile(name, [P, PACK, matrix.shape[1]], F32, after)
            queue.dma_start(raw[:], matrix.rearrange("(p j) c -> p j c", j=PACK))
            return raw

        def load_halves(name, matrix):
            return [load_rows("%s%d" % (name, h), matrix[:, 256 * h : 256 * (h + 1)], nc.sync) for h in range(2)]

        def load_by_row(name, column, queue):
            vec = tile(name, [P, PACK], F32)
            queue.dma_start(vec[:], column.rearrange("(p t) o -> p (t o)", t=PACK))
            return vec

        floor_arg = tile("floor_arg", [P, 1], F32)
        nc.gpsimd.memset(floor_arg[:], FLOOR_ARG)
        ident = tile("ident", [P, P], F32)
        make_identity(nc, ident[:])
        keys_pool_scales = load_scales("keys_scales", keys_scales)
        keys_pool = (load_words("keys_words", keys_words), keys_pool_scales)
        query_raw = load_rows("query_raw", query, nc.sync)
        th_sb = load_by_row("th_sb", th, nc.sync)
        tab_pool = (load_words("tab_words", tab_words), load_scales("tab_scales", tab_scales))
        w1_raw = load_rows("w1_raw", w1, nc.sync)
        sg_col = tile("sg_col", [P, 2], F32)
        nc.sync.dma_start(sg_col[:], sg.rearrange("o (p u) -> p (o u)", u=2))
        grows_raw = load_halves("grows_raw", grows)
        reserve_sb = load_by_row("reserve_sb", reserve, nc.sync)
        qs_sb = load_by_row("qs_sb", qs, nc.sync)
        gain_sb = tile("gain_sb", [P, 2, 2], F32)
        nc.sync.dma_start(gain_sb[:], gain.rearrange("(h p e) o -> p h (e o)", h=2, e=2))
        old_sb = tile("old_sb", [P, 2, 2 * I], F32)
        nc.sync.dma_start(old_sb[:], old.rearrange("(h p e) i -> p h (e i)", h=2, e=2))

        floor = tile("floor", [P, 1], F32)
        nc.scalar.activation(floor[:], floor_arg[:], ACT.Sigmoid)

        def gather(name, pool, dtype):
            listed = tile(name, [P, I], dtype)
            nc.vector.tensor_copy(listed[:], pool[:].indirect(offsets[:]))
            return listed

        keys_listed = (gather("keys_listed_words", keys_pool[0], U16), gather("keys_listed_scales", keys_pool[1], U8))

        query_bf = tile("query_bf", [P, PACK, P, PACK], BF16)
        dst = query_bf[:].rearrange("p t m j -> p m j t")
        src = query_raw[:].rearrange("p j (m t) -> p m j t", t=PACK)
        nc.vector.tensor_scalar(dst[:, :VECTOR_COLUMNS], src[:, :VECTOR_COLUMNS], -1.0, None, ALU.mult)
        nc.scalar.activation(dst[:, VECTOR_COLUMNS:], src[:, VECTOR_COLUMNS:], ACT.Copy, scale=-1.0)
        query_words = tile("query_words", [P, Q], U32)
        query_scales = tile("query_scales", [P, Q], U8)
        work = tile("work", [P, PACK, I], F32)
        scores = []
        for t in range(PACK):
            cols = slice(t * P, (t + 1) * P)
            nc.vector.quantize_mx(query_words[:, cols].bitcast(FP8X4), query_scales[:, cols], query_bf[:, t].rearrange("p m j -> p (m j)"))
            score = ps.tile([P, I], F32, name="score%d" % t)
            nc.tensor.matmul_mx(score[:], lhsT=query_words[:, cols].bitcast(FP8X4), lhsT_scale=query_scales[:, cols], rhs=keys_listed[0][:].bitcast(FP4X4), rhs_scale=keys_listed[1][:], start=True, stop=True)
            nc.scalar.activation(work[:, t, :], score[:], ACT.Sigmoid, bias=th_sb[:, t : t + 1])
            scores.append(score)

        tab_listed = (gather("tab_listed_words", tab_pool[0], U16), gather("tab_listed_scales", tab_pool[1], U8))

        def operand_tiles(name):
            return tile(name + "_bf", [P, 2, 2, P, PACK], BF16), tile(name + "_words", [P, R], U32), tile(name + "_scales", [P, R], U8)

        def cast_half(tiles, raw_half, h, copy):
            copy(
                tiles[0][:, h].rearrange("p e (c n) j -> p c j n e", n=2),
                raw_half.rearrange("p j (c n e) -> p c j n e", n=2, e=2),
            )

        def quantize_half(tiles, h):
            cols = slice(256 * h, 256 * (h + 1))
            nc.vector.quantize_mx(tiles[1][:, cols].bitcast(FP8X4), tiles[2][:, cols], tiles[0][:, h].rearrange("p e m j -> p (e m j)"))

        def product_half(bank, tiles, h, moving_words, moving_scales):
            for e in range(2):
                cols = slice(256 * h + P * e, 256 * h + P * (e + 1))
                nc.tensor.matmul_mx(bank[:, e, :], lhsT=tiles[1][:, cols].bitcast(FP8X4), lhsT_scale=tiles[2][:, cols], rhs=moving_words, rhs_scale=moving_scales, start=True, stop=True)

        w1_tiles = operand_tiles("w1")
        grows_tiles = operand_tiles("grows")
        for h in range(2):
            cast_half(w1_tiles, w1_raw[:, :, 256 * h : 256 * (h + 1)], h, nc.vector.tensor_copy)
        for h in range(2):
            quantize_half(w1_tiles, h)
        zh = []
        for h in range(2):
            bank = ps.tile([P, 2, I], F32, name="zh%d" % h)
            product_half(bank, w1_tiles, h, tab_listed[0][:].bitcast(FP4X4), tab_listed[1][:])
            zh.append(bank)

        log_outer = tile("log_outer", [P, 2, I], F32)
        nc.scalar.activation(log_outer[:], work[:, 0:4:3, :], ACT.Ln, bias=floor[:])
        nc.scalar.activation(work[:, 0:4:3, :], work[:, 1:3, :], ACT.Ln, bias=floor[:])
        logs = (log_outer[:, 0, :], work[:, 0, :], work[:, 3, :], log_outer[:, 1, :])

        cast_half(grows_tiles, grows_raw[0][:], 0, nc.vector.tensor_copy)
        cast_half(grows_tiles, grows_raw[1][:], 1, nc.scalar.copy)
        quantize_half(grows_tiles, 0)

        neg_p = tile("neg_p", [P, PACK, I], F32, "grows_raw0")
        neg_sum = tile("neg_sum", [P, PACK], F32)
        for t in (0, 3, 1, 2):
            nc.vector.scalar_tensor_tensor(neg_p[:, t, :], scores[t][:], th_sb[:, t : t + 1], logs[t], ALU.add, ALU.min, accum_out=neg_sum[:, t : t + 1])
        neg_z = tile("neg_z", [P, PACK], F32)
        nc.vector.tensor_tensor(neg_z[:], neg_sum[:], reserve_sb[:], ALU.subtract)
        neg_inv = tile("neg_inv", [P, PACK], F32)
        nc.vector.reciprocal(neg_inv[:], neg_z[:])
        neg_factor = tile("neg_factor", [P, PACK], F32)
        nc.vector.tensor_tensor(neg_factor[:], neg_inv[:], qs_sb[:], ALU.mult)

        wq_bf = tile("wq_bf", [P, I, PACK], BF16)
        wq_words = tile("wq_words", [P, I], U32)
        wq_scales = tile("wq_scales", [P, I], U8)
        for u in range(2):
            slots = slice(P * u, P * (u + 1))
            nc.vector.tensor_tensor(
                wq_bf[:, slots, :].rearrange("p (c n) t -> p c t n", n=4),
                neg_p[:, :, slots].rearrange("p t (c n) -> p c t n", n=4),
                neg_factor[:].unsqueeze(1).unsqueeze(3).to_broadcast([P, P // 4, PACK, 4]),
                ALU.mult,
            )
        for u in range(2):
            slots = slice(P * u, P * (u + 1))
            nc.vector.quantize_mx(wq_words[:, slots].bitcast(FP8X4), wq_scales[:, slots], wq_bf[:, slots, :].rearrange("p i t -> p (i t)"))
        quantize_half(grows_tiles, 1)

        sg_ps = ps.tile([P, 2, P], F32, name="sg_ps", tag="c0_0")
        for u in range(2):
            nc.tensor.transpose(sg_ps[:, u, :], sg_col[:, u : u + 1].to_broadcast([P, P]), ident[:])
        sg_rows = tile("sg_rows", [P, I], F32)
        nc.scalar.copy(sg_rows[:].rearrange("p (m u) -> p m u", u=2), sg_ps[:].rearrange("p u m -> p m u"))

        slope = tile("slope", [P, 2, 2 * I], F32, "grows_raw0")
        hts = tile("hts", [P, 2, 2, I], F32, "grows_raw1")
        squares = tile("squares", [P, 2, 2 * I], F32)
        for h in range(2):
            ht = hts[:, h]
            nc.scalar.activation(ht, zh[h][:], ACT.Tanh)
            nc.scalar.activation(squares[:, h, :].rearrange("p (e i) -> p e i", e=2), ht, ACT.Square)
            nc.vector.scalar_tensor_tensor(slope[:, h, :].rearrange("p (e i) -> p e i", e=2), squares[:, h, :].rearrange("p (e i) -> p e i", e=2), 1.0, sg_rows[:].unsqueeze(1).to_broadcast([P, 2, I]), ALU.subtract, ALU.mult)

        out_rows = out.rearrange("(h p e) i -> p h (e i)", h=2, e=2)
        term = tile("term", [P, 2, 2 * I], F32)
        result = tile("result", [P, 2, 2 * I], F32)
        for h in range(2):
            c0 = ps.tile([P, 2, I], F32, name="c0_%d" % h, tag="c0_%d" % h)
            product_half(c0, grows_tiles, h, wq_words[:].bitcast(FP8X4), wq_scales[:])
            for e in range(2):
                cols = slice(I * e, I * (e + 1))
                nc.vector.scalar_tensor_tensor(term[:, h, cols], c0[:, e, :], gain_sb[:, h, e : e + 1], slope[:, h, cols], ALU.mult, ALU.mult)
            for cols in ([slice(0, 2 * I)] if h == 0 else [slice(0, I), slice(I, 2 * I)]):
                nc.vector.tensor_tensor(result[:, h, cols], old_sb[:, h, cols], term[:, h, cols], ALU.subtract)
                nc.sync.dma_start(out_rows[:, h, cols], result[:, h, cols])
